import numpy as np
import ml_dtypes


def mxq(x, axis, fmt="e4m3"):
    dtype, down = {"e4m3": (ml_dtypes.float8_e4m3fn, 7), "e5m2": (ml_dtypes.float8_e5m2, 14)}[fmt]
    v = np.moveaxis(np.asarray(x, np.float32).astype(ml_dtypes.bfloat16).astype(np.float64), axis, -1)
    blocks = v.reshape(v.shape[:-1] + (-1, 32))
    amax = np.abs(blocks).max(-1, keepdims=True)
    byte = np.maximum(np.where(amax > 0, np.frexp(amax)[1] - 1 + 127, 0) - down, 1)
    scale = np.exp2(byte - 127.0)
    codes = (blocks / scale).astype(np.float32).astype(dtype).astype(np.float64)
    return np.moveaxis((codes * scale).reshape(v.shape), -1, axis)


WIDE = False


def mx_kscale(k):
    if not WIDE:
        return np.ones(k)
    levels = np.array([10, -10, 5, -5, 0])
    if k % 512:
        return np.exp2(np.random.permutation(np.resize(levels, k // 32))).repeat(32)
    a = np.empty((k // 512, 16))
    for p in range(k // 512):
        a[p, :8] = np.random.permutation(np.resize(levels, 8))
        for g in range(8):
            far = levels[np.abs(levels - a[p, g]) >= 10]
            a[p, g + 8] = far[np.random.randint(len(far))]
    return np.exp2(a.ravel()).repeat(32)


def f64(x):
    return np.asarray(x).astype(np.float64)


def striped(idx):
    return np.tile(idx.reshape(-1, 16).T, (8, 1)).astype(np.uint16)


def unstriped(offs):
    return offs[:16].T.reshape(-1).astype(np.int64)


E2M1 = np.array([0.0, 0.5, 1.0, 1.5, 2.0, 3.0, 4.0, 6.0, -0.0, -0.5, -1.0, -1.5, -2.0, -3.0, -4.0, -6.0])


def pack_weight(w, fmt):
    k, n = w.shape
    w = f64(np.asarray(w, np.float32).astype(ml_dtypes.bfloat16)).reshape(k // 32, 32, n)
    amax = np.abs(w).max(1)
    if fmt == "e4m3":
        byte = np.frexp(amax)[1] - 1 + 127 - 7
    else:
        mant, ex = np.frexp(amax / 6.0)
        byte = np.where(mant > 0.5, ex, ex - 1) + 127
    byte = np.clip(np.where(amax > 0, byte, 1), 1, 254)
    scaled = (w * np.exp2(127.0 - byte)[:, None, :]).reshape(k, n).astype(np.float32)
    by_word = np.ascontiguousarray(scaled.reshape(k // 512, 128, 4, n).transpose(0, 1, 3, 2))
    if fmt == "e4m3":
        words = by_word.astype(ml_dtypes.float8_e4m3fn).view(np.uint8)
    else:
        c = by_word.astype(ml_dtypes.float4_e2m1fn).view(np.uint8) & 0xF
        words = (c[..., 0::2] | (c[..., 1::2] << 4)).reshape(k // 512, 128, 2 * n)
    return np.ascontiguousarray(words), np.ascontiguousarray(byte.astype(np.uint8).reshape(k // 512, 16, n))


def unpack_weight(words, scales, fmt):
    g, _, n = scales.shape
    words = np.ascontiguousarray(words).reshape(g, 128, n, -1)
    if fmt == "e4m3":
        vals = words.view(ml_dtypes.float8_e4m3fn).astype(np.float64)
    else:
        nib = np.empty((g, 128, n, 4), np.uint8)
        nib[..., 0::2] = words & 0xF
        nib[..., 1::2] = words >> 4
        vals = E2M1[nib]
    vals = vals * np.repeat(np.exp2(scales.astype(np.float64) - 127.0), 8, axis=1)[..., None]
    return vals.transpose(0, 1, 3, 2).reshape(g * 512, n)


def gelu(v):
    return 0.5 * v * (1.0 + np.tanh(np.sqrt(2.0 / np.pi) * (v + 0.044715 * v**3)))


def striped8(idx):
    return np.concatenate([v.reshape(-1, 16).T for v in idx]).astype(np.uint16)


def unstriped8(offs):
    return np.stack([offs[16 * g:16 * g + 16].T.reshape(-1) for g in range(8)]).astype(np.int64)


def runs(v, idx8):
    k = np.arange(v.shape[0])
    return v[k[:, None], idx8[k % 512 // 64]]


K, KG, T, H, N, S, T2 = 1024, 512, 2048, 1024, 512, 1024, 2048

def setup_inputs():
    n = np.random.standard_normal
    s, sg, u = mx_kscale(K)[:, None], mx_kscale(KG)[:, None], mx_kscale(H)[:, None]
    tab_words, tab_scales = pack_weight(n((K, T)) * s, "e4m3")
    tab2_words, tab2_scales = pack_weight(n((KG, T)) * sg, "e4m3")
    wt_words, wt_scales = pack_weight(1.3 * n((K, H)) / np.sqrt(K) / s, "e2m1")
    wb_words, wb_scales = pack_weight(0.9 * n((KG, N)) / np.sqrt(KG) / sg, "e4m3")
    return {
        "tab_words": tab_words, "tab_scales": tab_scales,
        "tab2_words": tab2_words, "tab2_scales": tab2_scales,
        "offs": striped8(np.stack([np.random.permutation(T)[:S] for _ in range(8)])),
        "offs2": striped(np.random.permutation(T)[:S]),
        "offs3": striped(np.random.permutation(T2)[:S]),
        "wt_words": wt_words, "wt_scales": wt_scales,
        "wb_words": wb_words, "wb_scales": wb_scales,
        "wc": (0.52 * n((KG, H)) / np.sqrt(KG) / sg).astype(np.float32),
        "gain": (np.exp(0.3 * n(H)) * u[:, 0]).astype(np.float32),
        "wz": (1.6 * n((H, N)) / np.sqrt(H) / u).astype(np.float32),
        "bb": (0.5 * n(N)).astype(np.float32),
        "wgo": np.exp(0.3 * n((128, S))).astype(np.float32),
        "page1": n((N, T2)).astype(np.float32),
    }

def reference(tab_words, tab_scales, tab2_words, tab2_scales, offs, offs2, offs3, wt_words, wt_scales,
              wb_words, wb_scales, wc, gain, wz, bb, wgo, page1):
    v = runs(unpack_weight(tab_words, tab_scales, "e4m3"), unstriped8(offs))
    v2 = unpack_weight(tab2_words, tab2_scales, "e4m3")[:, unstriped(offs2)]
    wt = unpack_weight(wt_words, wt_scales, "e2m1")
    wb = unpack_weight(wb_words, wb_scales, "e4m3")
    test = np.tanh(wt.T @ v)
    gut = np.cos(mxq(f64(wc), 0, "e4m3").T @ v2)
    z = test * gut * f64(gain)[:, None]
    joint = mxq(f64(wz), 0, "e4m3").T @ mxq(z, 0, "e4m3")
    alone = (wb.T @ v2) + f64(bb)[:, None]
    y = np.maximum(joint, alone)
    out = f64(page1).copy()
    out[:, unstriped(offs3)] = np.tile(f64(wgo), (N // 128, 1)) * y
    return out

@@ -1,0 +1,235 @@
+from contextlib import ExitStack
+
+import concourse.mybir as mybir
+from concourse.masks import make_identity
+
+F32 = mybir.dt.float32
+BF16 = mybir.dt.bfloat16
+I32 = mybir.dt.int32
+U32 = mybir.dt.uint32
+U16 = mybir.dt.uint16
+U8 = mybir.dt.uint8
+FP8X4 = mybir.dt.float8_e4m3fn_x4
+FP4X4 = mybir.dt.float4_e2m1fn_x4
+ACT = mybir.ActivationFunctionType
+ALU = mybir.AluOpType
+
+FLOPS = 4831838208
+
+P = 128
+T = 2048
+S = 1024
+H = 1024
+N = 512
+W = 256
+SLICES = S // W
+OC = W // 16
+
+
+def tile_list_harp_string_adviser_kernel(
+    tc, tab_words, tab_scales, tab2_words, tab2_scales, offs, offs2, offs3, wt_words, wt_scales,
+    wb_words, wb_scales, wc, gain, wz, bb, wgo, page1, out,
+):
+    nc = tc.nc
+    with ExitStack() as ctx:
+        keep = ctx.enter_context(tc.tile_pool(name="keep", bufs=1))
+        ring = ctx.enter_context(tc.tile_pool(name="ring", bufs=3))
+        psum = ctx.enter_context(tc.psum_pool(name="psum", bufs=2))
+
+        def held(name, shape, dtype):
+            return keep.tile(shape, dtype, name=name, align_bytes=64)
+
+        lists8 = held("lists8", [P, S // 16], U16)
+        list2 = held("list2", [P, S // 16], U16)
+        list3 = held("list3", [P, S // 16], U16)
+        tab_sc = [held("tab_sc%d" % a, [P, T], U8) for a in range(2)]
+        tab2_sc = held("tab2_sc", [P, T], U8)
+        wt_sc_raw = held("wt_sc_raw", [P, 2 * H], U8)
+        wb_sc = held("wb_sc", [P, N], U8)
+        v_sc = held("v_sc", [P, 2, S], U8)
+        rows = held("rows", [P, P], F32)
+        ident = held("ident", [P, P], F32)
+
+        for a in range(2):
+            nc.vector.memset(tab_sc[a][:].bitcast(I32), 0)
+        warm = held("warm", [P, 1], F32)
+        nc.vector.memset(warm[:], 0.0)
+        nc.scalar.activation(warm[:], warm[:], ACT.Silu)
+        nc.vector.memset(tab2_sc[:].bitcast(I32), 0)
+        nc.vector.memset(wt_sc_raw[:].bitcast(I32), 0)
+        nc.gpsimd.memset(rows[:], 0.0)
+        nc.vector.memset(v_sc[:].rearrange("p a s -> p (a s)").bitcast(I32), 0)
+        nc.vector.memset(wb_sc[:].bitcast(I32), 0)
+
+        for b in range(2):
+            nc.gpsimd.dma_start(
+                out=rows[4 * b : 4 * b + 4, :].rearrange("t (u e) -> t u e", e=4),
+                in_=gain[512 * b : 512 * (b + 1)].rearrange("(u t e) -> t u e", t=4, e=4))
+        nc.gpsimd.dma_start(out=rows[8:12, :], in_=bb.rearrange("(i p) -> i p", p=P))
+        make_identity(nc, ident[:])
+        nc.sync.dma_start(lists8[:], offs)
+        nc.sync.dma_start(list2[:], offs2)
+        for a in range(2):
+            nc.scalar.dma_start(out=tab_sc[a][:].bitcast(I32)[0:P:8, :], in_=tab_scales[a].bitcast(I32))
+        tab2_w = held("tab2_w", [P, T], I32)
+        nc.sync.dma_start(out=tab2_w[:], in_=tab2_words[0].rearrange("p n t -> p (n t)").bitcast(I32))
+        for d in range(4):
+            nc.scalar.dma_start(out=tab2_sc[:].bitcast(I32)[32 * d : 32 * d + 4, :],
+                                in_=tab2_scales[0, 4 * d : 4 * d + 4, :].bitcast(I32))
+        wt_raw = held("wt_raw", [P, 2, H // 2], I32)
+        nc.sync.dma_start(out=wt_raw[:], in_=wt_words.bitcast(I32).rearrange("a p w -> p a w"))
+        for d in range(4):
+            nc.scalar.dma_start(
+                out=wt_sc_raw[:].bitcast(I32)[32 * d : 32 * d + 4, :].rearrange("p (a w) -> p a w", a=2),
+                in_=wt_scales.bitcast(I32)[:, 4 * d : 4 * d + 4, :].rearrange("a r w -> r a w"))
+        wc_raw = [held("wc_raw%d" % b, [P, 4, 512], F32) for b in range(2)]
+        wc_rows = wc.rearrange("(p j) c -> p j c", j=4)
+        nc.sync.dma_start(out=wc_raw[0][:], in_=wc_rows[:, :, 0:512])
+        tab_w = [held("tab_w%d" % a, [P, T], I32) for a in range(2)]
+        for a in range(2):
+            nc.sync.dma_start(out=tab_w[a][:], in_=tab_words[a].rearrange("p n t -> p (n t)").bitcast(I32))
+        nc.sync.dma_start(out=wc_raw[1][:], in_=wc_rows[:, :, 512:1024])
+
+        tab_sc_g = held("tab_sc_g", [P, 2, S], U8)
+        for a in range(2):
+            nc.vector.tensor_copy(tab_sc_g[:, a, :], tab_sc[a][:].indirect(lists8[:]))
+        v2_sc = held("v2_sc", [P, S], U8)
+        nc.vector.tensor_copy(v2_sc[:], tab2_sc[:].indirect(list2[:]))
+        for r in range(4):
+            nc.gpsimd.dma_start(out=v_sc[:].rearrange("p a s -> p (a s)").bitcast(I32)[r:P:32, :],
+                                in_=tab_sc_g[:].rearrange("p a s -> p (a s)").bitcast(I32)[8 * r : P : 32, :])
+
+        wb_w = held("wb_w", [P, N], I32)
+        nc.sync.dma_start(out=wb_w[:], in_=wb_words[0].rearrange("p n t -> p (n t)").bitcast(I32))
+        for d in range(4):
+            nc.sync.dma_start(out=wb_sc[:].bitcast(I32)[32 * d : 32 * d + 4, :],
+                                in_=wb_scales[0, 4 * d : 4 * d + 4, :].bitcast(I32))
+        nc.sync.dma_start(list3[:], offs3)
+        wz_raw = [held("wz_raw%d" % b, [P, 4, N], F32) for b in range(2)]
+        for b in range(2):
+            wz_rows = wz[512 * b : 512 * (b + 1), :].rearrange("(u t e) n -> e u t n", t=4, e=4)
+            for e in range(4):
+                nc.sync.dma_start(out=wz_raw[b][e:P:4, :, :], in_=wz_rows[e])
+        wgo_sb = held("wgo_sb", [P, S], F32)
+        nc.sync.dma_start(out=wgo_sb[:], in_=wgo)
+        page = [held("page%d" % i, [P, T], F32) for i in range(4)]
+        for i in range(4):
+            nc.sync.dma_start(out=page[i][:], in_=page1[P * i : P * (i + 1), :])
+
+        wt_w = held("wt_w", [P, 2 * H // 2], U32)
+        nc.scalar.copy(out=wt_w[:].rearrange("p (ab t u w) -> p ab t u w", ab=4, t=4, w=2),
+                       in_=wt_raw[:].bitcast(U32).rearrange("p a (b u t w) -> p (a b) t u w", b=2, t=4, w=2))
+        wt_sc = held("wt_sc", [P, 2 * H], U8)
+        nc.scalar.copy(out=wt_sc[:].bitcast(U32).rearrange("p (ab t u) -> p ab u t", ab=4, t=4),
+                       in_=wt_sc_raw[:].bitcast(U32).rearrange("p (ab u t) -> p ab u t", ab=4, t=4))
+
+        turned = psum.tile([P, 2, W], F32, name="alone_sum")
+        nc.tensor.transpose(turned[:, 0, 0:P], rows[:], ident[:])
+        cols = held("cols", [P, 12], F32)
+        nc.scalar.copy(cols[:], turned[:, 0, 0:12])
+        gain_m2 = held("gain_m2", [P, 8], F32)
+        nc.scalar.activation(gain_m2[:], turned[:, 0, 0:8], ACT.Copy, scale=-2.0)
+
+        def quantise(name, pool, grouped, width):
+            codes = pool.tile([P, width], U32, name=name + "_w", align_bytes=64)
+            scales = pool.tile([P, width], U8, name=name + "_sc", align_bytes=64)
+            nc.vector.quantize_mx(out=codes[:].bitcast(FP8X4), scales=scales[:], in_=grouped)
+            return codes, scales
+
+        def prepare_wc(b, copy):
+            grouped = held("wc_bf%d" % b, [P, 2048], BF16)
+            copy(out=grouped[:].rearrange("p (t u e j) -> p t u j e", t=4, e=4, j=4),
+                 in_=wc_raw[b][:].rearrange("p j (u t e) -> p t u j e", t=4, e=4))
+            return quantise("wc%d" % b, keep, grouped[:], 512)
+
+        def prepare_wz(b):
+            grouped = held("wz_bf%d" % b, [P, 2048], BF16)
+            nc.vector.tensor_copy(out=grouped[:].rearrange("p (c i t) -> p c t i", i=4, t=4),
+                                  in_=wz_raw[b][:].rearrange("p t (c i) -> p c t i", i=4))
+            return quantise("wz%d" % b, keep, grouped[:], 512)
+
+        def gather_words(name, window, offsets, s):
+            picked = held("%s_%d" % (name, s), [P, W], U32)
+            nc.vector.tensor_copy(picked[:], window[:].bitcast(U32).indirect(offsets[:, OC * s : OC * (s + 1)]))
+            return picked
+
+        v2_w, v_w = {}, {}
+        v2_w[0] = gather_words("v2", tab2_w, list2, 0)
+        wc_q = [prepare_wc(0, nc.scalar.copy)]
+        for s in range(1, SLICES):
+            v2_w[s] = gather_words("v2", tab2_w, list2, s)
+        for a in range(2):
+            v_w[a, 0] = gather_words("v%d" % a, tab_w[a], lists8, 0)
+        wc_q.append(prepare_wc(1, nc.vector.tensor_copy))
+        for s in range(1, SLICES):
+            for a in range(2):
+                v_w[a, s] = gather_words("v%d" % a, tab_w[a], lists8, s)
+        wz_q = [prepare_wz(b) for b in range(2)]
+
+        def mx(acc, codes, scales, col, rhs, rhs_scale, start, stop):
+            nc.tensor.matmul_mx(out=acc, lhsT=codes, lhsT_scale=scales[:, col : col + P], rhs=rhs[:].bitcast(FP8X4),
+                                rhs_scale=rhs_scale, start=start, stop=stop)
+
+        def first_stage(s, b):
+            js = slice(W * s, W * (s + 1))
+            test = ring.tile([P, 4, W], F32, name="test")
+            gut = ring.tile([P, 4, W], F32, name="gut")
+            for h in range(2):
+                acc = psum.tile([P, 2, W], F32, name="gut_sum", bufs=4)
+                for tt in range(2):
+                    col = P * (2 * h + tt)
+                    mx(acc[:, tt, :], wc_q[b][0][:, col : col + P].bitcast(FP8X4), wc_q[b][1], col,
+                       v2_w[s], v2_sc[:, js], True, True)
+                nc.scalar.activation(gut[:, 2 * h : 2 * h + 2, :], acc[:], ACT.Sin, scale=0.5)
+            nc.scalar.activation(gut[:], gut[:], ACT.Square)
+            for t in range(4):
+                c = 4 * b + t
+                nc.scalar.activation(gut[:, t, :], gut[:, t, :], ACT.Identity,
+                                     bias=cols[:, c : c + 1], scale=gain_m2[:, c : c + 1])
+            for h in range(2):
+                acc = psum.tile([P, 2, W], F32, name="test_sum")
+                for tt in range(2):
+                    for a in range(2):
+                        col = H * a + 512 * b + P * (2 * h + tt)
+                        mx(acc[:, tt, :], wt_w[:].bitcast(U8)[:, 2 * col : 2 * (col + P)].bitcast(FP4X4), wt_sc, col,
+                           v_w[a, s], v_sc[:, a, js], a == 0, a == 1)
+                nc.scalar.activation(test[:, 2 * h : 2 * h + 2, :], acc[:], ACT.Tanh)
+            z = ring.tile([P, 4 * W], BF16, name="z", align_bytes=64)
+            nc.vector.tensor_tensor(z[:].rearrange("p (c i t) -> p c t i", i=2, t=4),
+                                    test[:].rearrange("p t (c i) -> p c t i", i=2),
+                                    gut[:].rearrange("p t (c i) -> p c t i", i=2), ALU.mult)
+            return quantise("z%d" % b, ring, z[:], W)
+
+        def second_stage(s, h, z_q):
+            js = slice(W * s, W * (s + 1))
+            if True:
+                acc = psum.tile([P, 2, W], F32, name="alone_sum")
+                alone = ring.tile([P, 2, W], F32, name="alone")
+                for nn in range(2):
+                    col = P * (2 * h + nn)
+                    mx(acc[:, nn, :], wb_w[:, col : col + P].bitcast(FP8X4), wb_sc, col, v2_w[s], v2_sc[:, js], True, True)
+                for nn in range(2):
+                    c = 8 + 2 * h + nn
+                    nc.scalar.activation(alone[:, nn, :], acc[:, nn, :], ACT.Identity, bias=cols[:, c : c + 1])
+                joint = psum.tile([P, 2, W], F32, name="test_sum")
+                for nn in range(2):
+                    col = P * (2 * h + nn)
+                    for b in range(2):
+                        mx(joint[:, nn, :], wz_q[b][0][:, col : col + P].bitcast(FP8X4), wz_q[b][1], col,
+                           z_q[b][0], z_q[b][1][:], b == 0, b == 1)
+                y = ring.tile([P, 2, W], F32, name="y")
+                nc.vector.tensor_tensor(y[:], joint[:], alone[:], ALU.max)
+                for nn in range(2):
+                    i = 2 * h + nn
+                    nc.vector.tensor_tensor(page[i][:].indirect(list3[:, OC * s : OC * (s + 1)]),
+                                            y[:, nn, :], wgo_sb[:, js], ALU.mult)
+                    if s == SLICES - 1:
+                        nc.sync.dma_start(out=out[P * i : P * (i + 1), :], in_=page[i][:])
+
+        z_q = []
+        for k in range(2 * SLICES + 2):
+            if k < 2 * SLICES:
+                z_q.append(first_stage(k // 2, k % 2))
+            if k >= 2:
+                s = (k - 2) // 2
+                second_stage(s, k % 2, z_q[2 * s : 2 * s + 2])

@@ -24,6 +24,7 @@ N = 512
 W = 256
 SLICES = S // W
 OC = W // 16
+LAG = 1
 
 
 def tile_list_harp_string_adviser_kernel(
@@ -46,59 +47,60 @@ def tile_list_harp_string_adviser_kernel(
         tab2_sc = held("tab2_sc", [P, T], U8)
         wt_sc_raw = held("wt_sc_raw", [P, 2 * H], U8)
         wb_sc = held("wb_sc", [P, N], U8)
-        v_sc = held("v_sc", [P, 2, S], U8)
+        v_sc = [held("v_sc%d" % f, [P, 2, S // 2], U8) for f in range(2)]
         rows = held("rows", [P, P], F32)
         ident = held("ident", [P, P], F32)
 
-        for a in range(2):
-            nc.vector.memset(tab_sc[a][:].bitcast(I32), 0)
         warm = held("warm", [P, 1], F32)
         nc.vector.memset(warm[:], 0.0)
         nc.scalar.activation(warm[:], warm[:], ACT.Silu)
+        nc.vector.memset(tab_sc[0][:].bitcast(I32), 0)
+        nc.gpsimd.memset(tab_sc[1][:].bitcast(I32), 0)
         nc.vector.memset(tab2_sc[:].bitcast(I32), 0)
-        nc.vector.memset(wt_sc_raw[:].bitcast(I32), 0)
+        nc.gpsimd.memset(wt_sc_raw[:].bitcast(I32), 0)
         nc.gpsimd.memset(rows[:], 0.0)
-        nc.vector.memset(v_sc[:].rearrange("p a s -> p (a s)").bitcast(I32), 0)
         nc.vector.memset(wb_sc[:].bitcast(I32), 0)
 
-        for b in range(2):
-            nc.gpsimd.dma_start(
-                out=rows[4 * b : 4 * b + 4, :].rearrange("t (u e) -> t u e", e=4),
-                in_=gain[512 * b : 512 * (b + 1)].rearrange("(u t e) -> t u e", t=4, e=4))
-        nc.gpsimd.dma_start(out=rows[8:12, :], in_=bb.rearrange("(i p) -> i p", p=P))
         make_identity(nc, ident[:])
+        for f in range(2):
+            nc.vector.memset(v_sc[f][:].rearrange("p a s -> p (a s)").bitcast(I32), 0)
         nc.sync.dma_start(lists8[:], offs)
-        nc.sync.dma_start(list2[:], offs2)
         for a in range(2):
-            nc.scalar.dma_start(out=tab_sc[a][:].bitcast(I32)[0:P:8, :], in_=tab_scales[a].bitcast(I32))
+            nc.sync.dma_start(out=tab_sc[a][:].bitcast(I32)[0:P:8, :], in_=tab_scales[a].bitcast(I32))
+        nc.sync.dma_start(list2[:], offs2)
         tab2_w = held("tab2_w", [P, T], I32)
         nc.sync.dma_start(out=tab2_w[:], in_=tab2_words[0].rearrange("p n t -> p (n t)").bitcast(I32))
         for d in range(4):
             nc.scalar.dma_start(out=tab2_sc[:].bitcast(I32)[32 * d : 32 * d + 4, :],
                                 in_=tab2_scales[0, 4 * d : 4 * d + 4, :].bitcast(I32))
-        wt_raw = held("wt_raw", [P, 2, H // 2], I32)
-        nc.sync.dma_start(out=wt_raw[:], in_=wt_words.bitcast(I32).rearrange("a p w -> p a w"))
-        for d in range(4):
+        for b in range(2):
             nc.scalar.dma_start(
-                out=wt_sc_raw[:].bitcast(I32)[32 * d : 32 * d + 4, :].rearrange("p (a w) -> p a w", a=2),
-                in_=wt_scales.bitcast(I32)[:, 4 * d : 4 * d + 4, :].rearrange("a r w -> r a w"))
+                out=rows[4 * b : 4 * b + 4, :].rearrange("t (u e) -> t u e", e=4),
+                in_=gain[512 * b : 512 * (b + 1)].rearrange("(u t e) -> t u e", t=4, e=4))
+        nc.scalar.dma_start(out=rows[8:12, :], in_=bb.rearrange("(i p) -> i p", p=P))
         wc_raw = [held("wc_raw%d" % b, [P, 4, 512], F32) for b in range(2)]
         wc_rows = wc.rearrange("(p j) c -> p j c", j=4)
         nc.sync.dma_start(out=wc_raw[0][:], in_=wc_rows[:, :, 0:512])
+        for d in range(4):
+            nc.gpsimd.dma_start(
+                out=wt_sc_raw[:].bitcast(I32)[32 * d : 32 * d + 4, :].rearrange("p (a w) -> p a w", a=2),
+                in_=wt_scales.bitcast(I32)[:, 4 * d : 4 * d + 4, :].rearrange("a r w -> r a w"))
         tab_w = [held("tab_w%d" % a, [P, T], I32) for a in range(2)]
         for a in range(2):
             nc.sync.dma_start(out=tab_w[a][:], in_=tab_words[a].rearrange("p n t -> p (n t)").bitcast(I32))
+        wt_raw = held("wt_raw", [P, 2, H // 2], I32)
+        nc.sync.dma_start(out=wt_raw[:], in_=wt_words.bitcast(I32).rearrange("a p w -> p a w"))
         nc.sync.dma_start(out=wc_raw[1][:], in_=wc_rows[:, :, 512:1024])
 
-        tab_sc_g = held("tab_sc_g", [P, 2, S], U8)
-        for a in range(2):
-            nc.vector.tensor_copy(tab_sc_g[:, a, :], tab_sc[a][:].indirect(lists8[:]))
-        v2_sc = held("v2_sc", [P, S], U8)
-        nc.vector.tensor_copy(v2_sc[:], tab2_sc[:].indirect(list2[:]))
-        for r in range(4):
-            nc.gpsimd.dma_start(out=v_sc[:].rearrange("p a s -> p (a s)").bitcast(I32)[r:P:32, :],
-                                in_=tab_sc_g[:].rearrange("p a s -> p (a s)").bitcast(I32)[8 * r : P : 32, :])
+        def tab_scale_half(f, queue):
+            picked = held("tab_sc_g%d" % f, [P, 2, S // 2], U8)
+            for a in range(2):
+                nc.vector.tensor_copy(picked[:, a, :], tab_sc[a][:].indirect(lists8[:, 2 * OC * f : 2 * OC * (f + 1)]))
+            for r in range(4):
+                queue.dma_start(out=v_sc[f][:].rearrange("p a s -> p (a s)").bitcast(I32)[r:P:32, :],
+                                in_=picked[:].rearrange("p a s -> p (a s)").bitcast(I32)[8 * r : P : 32, :])
 
+        tab_scale_half(0, nc.scalar)
         wb_w = held("wb_w", [P, N], I32)
         nc.sync.dma_start(out=wb_w[:], in_=wb_words[0].rearrange("p n t -> p (n t)").bitcast(I32))
         for d in range(4):
@@ -106,7 +108,7 @@ def tile_list_harp_string_adviser_kernel(
                                 in_=wb_scales[0, 4 * d : 4 * d + 4, :].bitcast(I32))
         nc.sync.dma_start(list3[:], offs3)
         wz_raw = [held("wz_raw%d" % b, [P, 4, N], F32) for b in range(2)]
-        for b in range(2):
+        for b in (1, 0):
             wz_rows = wz[512 * b : 512 * (b + 1), :].rearrange("(u t e) n -> e u t n", t=4, e=4)
             for e in range(4):
                 nc.sync.dma_start(out=wz_raw[b][e:P:4, :, :], in_=wz_rows[e])
@@ -115,20 +117,6 @@ def tile_list_harp_string_adviser_kernel(
         page = [held("page%d" % i, [P, T], F32) for i in range(4)]
         for i in range(4):
             nc.sync.dma_start(out=page[i][:], in_=page1[P * i : P * (i + 1), :])
-
-        wt_w = held("wt_w", [P, 2 * H // 2], U32)
-        nc.scalar.copy(out=wt_w[:].rearrange("p (ab t u w) -> p ab t u w", ab=4, t=4, w=2),
-                       in_=wt_raw[:].bitcast(U32).rearrange("p a (b u t w) -> p (a b) t u w", b=2, t=4, w=2))
-        wt_sc = held("wt_sc", [P, 2 * H], U8)
-        nc.scalar.copy(out=wt_sc[:].bitcast(U32).rearrange("p (ab t u) -> p ab u t", ab=4, t=4),
-                       in_=wt_sc_raw[:].bitcast(U32).rearrange("p (ab u t) -> p ab u t", ab=4, t=4))
-
-        turned = psum.tile([P, 2, W], F32, name="alone_sum")
-        nc.tensor.transpose(turned[:, 0, 0:P], rows[:], ident[:])
-        cols = held("cols", [P, 12], F32)
-        nc.scalar.copy(cols[:], turned[:, 0, 0:12])
-        gain_m2 = held("gain_m2", [P, 8], F32)
-        nc.scalar.activation(gain_m2[:], turned[:, 0, 0:8], ACT.Copy, scale=-2.0)
 
         def quantise(name, pool, grouped, width):
             codes = pool.tile([P, width], U32, name=name + "_w", align_bytes=64)
@@ -143,28 +131,52 @@ def tile_list_harp_string_adviser_kernel(
             return quantise("wc%d" % b, keep, grouped[:], 512)
 
         def prepare_wz(b):
-            grouped = held("wz_bf%d" % b, [P, 2048], BF16)
+            grouped = ring.tile([P, 2048], BF16, name="wz_bf", tag="turns", align_bytes=64)
             nc.vector.tensor_copy(out=grouped[:].rearrange("p (c i t) -> p c t i", i=4, t=4),
                                   in_=wz_raw[b][:].rearrange("p t (c i) -> p c t i", i=4))
             return quantise("wz%d" % b, keep, grouped[:], 512)
 
         def gather_words(name, window, offsets, s):
-            picked = held("%s_%d" % (name, s), [P, W], U32)
+            picked = ring.tile([P, W], U32, name=name, bufs=2, align_bytes=64)
             nc.vector.tensor_copy(picked[:], window[:].bitcast(U32).indirect(offsets[:, OC * s : OC * (s + 1)]))
             return picked
 
-        v2_w, v_w = {}, {}
+        def gather_scales(s):
+            picked = ring.tile([P, W], U8, name="v2_sc", bufs=2, align_bytes=64)
+            nc.vector.tensor_copy(picked[:], tab2_sc[:].indirect(list2[:, OC * s : OC * (s + 1)]))
+            return picked
+
+        v2_w, v_w, v2_sc = {}, {}, {}
+        v2_sc[0] = gather_scales(0)
         v2_w[0] = gather_words("v2", tab2_w, list2, 0)
         wc_q = [prepare_wc(0, nc.scalar.copy)]
-        for s in range(1, SLICES):
-            v2_w[s] = gather_words("v2", tab2_w, list2, s)
+        wt_w = held("wt_w", [P, 2 * H // 2], I32)
+        nc.vector.tensor_copy(out=wt_w[:].rearrange("p (ab t u w) -> p ab t u w", ab=4, t=4, w=2),
+                       in_=wt_raw[:].rearrange("p a (b u t w) -> p (a b) t u w", b=2, t=4, w=2))
+        wt_sc = held("wt_sc", [P, 2 * H], U8)
+        nc.vector.tensor_copy(out=wt_sc[:].bitcast(I32).rearrange("p (ab t u) -> p ab u t", ab=4, t=4),
+                       in_=wt_sc_raw[:].bitcast(I32).rearrange("p (ab u t) -> p ab u t", ab=4, t=4))
+
+        turned = psum.tile([P, 2, W], F32, name="alone_sum")
+        nc.tensor.transpose(turned[:, 0, 0:P], rows[:], ident[:])
+        cols = held("cols", [P, 12], F32)
+        nc.scalar.copy(cols[:], turned[:, 0, 0:12])
+        gain_m2 = held("gain_m2", [P, 8], F32)
+        nc.scalar.activation(gain_m2[:], turned[:, 0, 0:8], ACT.Copy, scale=-2.0)
+
         for a in range(2):
             v_w[a, 0] = gather_words("v%d" % a, tab_w[a], lists8, 0)
         wc_q.append(prepare_wc(1, nc.vector.tensor_copy))
-        for s in range(1, SLICES):
+
+        def gather_slice(s):
+            v2_sc[s] = gather_scales(s)
+            v2_w[s] = gather_words("v2", tab2_w, list2, s)
             for a in range(2):
                 v_w[a, s] = gather_words("v%d" % a, tab_w[a], lists8, s)
-        wz_q = [prepare_wz(b) for b in range(2)]
+
+        gather_slice(1)
+        tab_scale_half(1, nc.gpsimd)
+        wz_q = []
 
         def mx(acc, codes, scales, col, rhs, rhs_scale, start, stop):
             nc.tensor.matmul_mx(out=acc, lhsT=codes, lhsT_scale=scales[:, col : col + P], rhs=rhs[:].bitcast(FP8X4),
@@ -175,11 +187,11 @@ def tile_list_harp_string_adviser_kernel(
             test = ring.tile([P, 4, W], F32, name="test")
             gut = ring.tile([P, 4, W], F32, name="gut")
             for h in range(2):
-                acc = psum.tile([P, 2, W], F32, name="gut_sum", bufs=4)
+                acc = psum.tile([P, 2, W], F32, name="gut_sum", tag="sums", bufs=6)
                 for tt in range(2):
                     col = P * (2 * h + tt)
                     mx(acc[:, tt, :], wc_q[b][0][:, col : col + P].bitcast(FP8X4), wc_q[b][1], col,
-                       v2_w[s], v2_sc[:, js], True, True)
+                       v2_w[s], v2_sc[s][:], True, True)
                 nc.scalar.activation(gut[:, 2 * h : 2 * h + 2, :], acc[:], ACT.Sin, scale=0.5)
             nc.scalar.activation(gut[:], gut[:], ACT.Square)
             for t in range(4):
@@ -187,37 +199,43 @@ def tile_list_harp_string_adviser_kernel(
                 nc.scalar.activation(gut[:, t, :], gut[:, t, :], ACT.Identity,
                                      bias=cols[:, c : c + 1], scale=gain_m2[:, c : c + 1])
             for h in range(2):
-                acc = psum.tile([P, 2, W], F32, name="test_sum")
+                acc = psum.tile([P, 2, W], F32, name="test_sum", tag="sums", bufs=6)
                 for tt in range(2):
                     for a in range(2):
                         col = H * a + 512 * b + P * (2 * h + tt)
                         mx(acc[:, tt, :], wt_w[:].bitcast(U8)[:, 2 * col : 2 * (col + P)].bitcast(FP4X4), wt_sc, col,
-                           v_w[a, s], v_sc[:, a, js], a == 0, a == 1)
+                           v_w[a, s], v_sc[s // 2][:, a, W * (s % 2) : W * (s % 2 + 1)], a == 0, a == 1)
                 nc.scalar.activation(test[:, 2 * h : 2 * h + 2, :], acc[:], ACT.Tanh)
-            z = ring.tile([P, 4 * W], BF16, name="z", align_bytes=64)
+            if (s, b) == (0, 0):
+                z = held("wc_bf1", [P, 4 * W], BF16)
+            else:
+                z = ring.tile([P, 4 * W], BF16, name="z", tag="turns", align_bytes=64)
             nc.vector.tensor_tensor(z[:].rearrange("p (c i t) -> p c t i", i=2, t=4),
                                     test[:].rearrange("p t (c i) -> p c t i", i=2),
                                     gut[:].rearrange("p t (c i) -> p c t i", i=2), ALU.mult)
             return quantise("z%d" % b, ring, z[:], W)
 
-        def second_stage(s, h, z_q):
+        def alone_scores(s, h):
+            acc = psum.tile([P, 2, W], F32, name="alone_sum")
+            alone = ring.tile([P, 2, W], F32, name="alone", bufs=4)
+            for nn in range(2):
+                col = P * (2 * h + nn)
+                mx(acc[:, nn, :], wb_w[:, col : col + P].bitcast(FP8X4), wb_sc, col, v2_w[s], v2_sc[s][:], True, True)
+            for nn in range(2):
+                c = 8 + 2 * h + nn
+                nc.scalar.activation(alone[:, nn, :], acc[:, nn, :], ACT.Identity, bias=cols[:, c : c + 1])
+            return alone
+
+        def second_stage(s, h, z_q, alone):
             js = slice(W * s, W * (s + 1))
             if True:
-                acc = psum.tile([P, 2, W], F32, name="alone_sum")
-                alone = ring.tile([P, 2, W], F32, name="alone")
-                for nn in range(2):
-                    col = P * (2 * h + nn)
-                    mx(acc[:, nn, :], wb_w[:, col : col + P].bitcast(FP8X4), wb_sc, col, v2_w[s], v2_sc[:, js], True, True)
-                for nn in range(2):
-                    c = 8 + 2 * h + nn
-                    nc.scalar.activation(alone[:, nn, :], acc[:, nn, :], ACT.Identity, bias=cols[:, c : c + 1])
-                joint = psum.tile([P, 2, W], F32, name="test_sum")
+                joint = psum.tile([P, 2, W], F32, name="joint", tag="sums", bufs=6)
                 for nn in range(2):
                     col = P * (2 * h + nn)
                     for b in range(2):
                         mx(joint[:, nn, :], wz_q[b][0][:, col : col + P].bitcast(FP8X4), wz_q[b][1], col,
                            z_q[b][0], z_q[b][1][:], b == 0, b == 1)
-                y = ring.tile([P, 2, W], F32, name="y")
+                y = ring.tile([P, 2, W], F32, name="y", tag="turns", align_bytes=64)
                 nc.vector.tensor_tensor(y[:], joint[:], alone[:], ALU.max)
                 for nn in range(2):
                     i = 2 * h + nn
@@ -226,10 +244,15 @@ def tile_list_harp_string_adviser_kernel(
                     if s == SLICES - 1:
                         nc.sync.dma_start(out=out[P * i : P * (i + 1), :], in_=page[i][:])
 
-        z_q = []
-        for k in range(2 * SLICES + 2):
+        z_q, alones = [], []
+        for k in range(2 * SLICES + LAG):
             if k < 2 * SLICES:
                 z_q.append(first_stage(k // 2, k % 2))
-            if k >= 2:
-                s = (k - 2) // 2
-                second_stage(s, k % 2, z_q[2 * s : 2 * s + 2])
+                alones.append(alone_scores(k // 2, k % 2))
+                if k == 1:
+                    wz_q.extend(prepare_wz(b) for b in range(2))
+                if k in (1, 3):
+                    gather_slice((k + 3) // 2)
+            if k >= LAG:
+                s = (k - LAG) // 2
+                second_stage(s, (k - LAG) % 2, z_q[2 * s : 2 * s + 2], alones[k - LAG])

@@ -210,9 +210,9 @@ def tile_list_harp_string_adviser_kernel(
                 z = held("wc_bf1", [P, 4 * W], BF16)
             else:
                 z = ring.tile([P, 4 * W], BF16, name="z", tag="turns", align_bytes=64)
-            nc.vector.tensor_tensor(z[:].rearrange("p (c i t) -> p c t i", i=2, t=4),
-                                    test[:].rearrange("p t (c i) -> p c t i", i=2),
-                                    gut[:].rearrange("p t (c i) -> p c t i", i=2), ALU.mult)
+            nc.vector.tensor_tensor(z[:].rearrange("p (c i t) -> p c t i", i=4, t=4),
+                                    test[:].rearrange("p t (c i) -> p c t i", i=4),
+                                    gut[:].rearrange("p t (c i) -> p c t i", i=4), ALU.mult)
             return quantise("z%d" % b, ring, z[:], W)
 
         def alone_scores(s, h):

@@ -24,7 +24,6 @@ N = 512
 W = 256
 SLICES = S // W
 OC = W // 16
-LAG = 1
 
 
 def tile_list_harp_string_adviser_kernel(
@@ -131,7 +130,7 @@ def tile_list_harp_string_adviser_kernel(
             return quantise("wc%d" % b, keep, grouped[:], 512)
 
         def prepare_wz(b):
-            grouped = ring.tile([P, 2048], BF16, name="wz_bf", tag="turns", align_bytes=64)
+            grouped = ring.tile([P, 2048], BF16, name="wz_bf", tag="turns", bufs=2, align_bytes=64)
             nc.vector.tensor_copy(out=grouped[:].rearrange("p (c i t) -> p c t i", i=4, t=4),
                                   in_=wz_raw[b][:].rearrange("p t (c i) -> p c t i", i=4))
             return quantise("wz%d" % b, keep, grouped[:], 512)
@@ -154,8 +153,8 @@ def tile_list_harp_string_adviser_kernel(
         nc.vector.tensor_copy(out=wt_w[:].rearrange("p (ab t u w) -> p ab t u w", ab=4, t=4, w=2),
                        in_=wt_raw[:].rearrange("p a (b u t w) -> p (a b) t u w", b=2, t=4, w=2))
         wt_sc = held("wt_sc", [P, 2 * H], U8)
-        nc.vector.tensor_copy(out=wt_sc[:].bitcast(I32).rearrange("p (ab t u) -> p ab u t", ab=4, t=4),
-                       in_=wt_sc_raw[:].bitcast(I32).rearrange("p (ab u t) -> p ab u t", ab=4, t=4))
+        nc.vector.tensor_copy(out=wt_sc[:].bitcast(I32).rearrange("p (ab t u) -> p ab t u", ab=4, t=4),
+                       in_=wt_sc_raw[:].bitcast(I32).rearrange("p (ab u t) -> p ab t u", ab=4, t=4))
 
         turned = psum.tile([P, 2, W], F32, name="alone_sum")
         nc.tensor.transpose(turned[:, 0, 0:P], rows[:], ident[:])
@@ -186,8 +185,10 @@ def tile_list_harp_string_adviser_kernel(
             js = slice(W * s, W * (s + 1))
             test = ring.tile([P, 4, W], F32, name="test")
             gut = ring.tile([P, 4, W], F32, name="gut")
+            test_sums = [psum.tile([P, 2, W], F32, name="test_sum", tag="sums", bufs=6) for h in range(2)]
+            gut_sums = [psum.tile([P, 2, W], F32, name="gut_sum", tag="sums", bufs=6) for h in range(2)]
             for h in range(2):
-                acc = psum.tile([P, 2, W], F32, name="gut_sum", tag="sums", bufs=6)
+                acc = gut_sums[h]
                 for tt in range(2):
                     col = P * (2 * h + tt)
                     mx(acc[:, tt, :], wc_q[b][0][:, col : col + P].bitcast(FP8X4), wc_q[b][1], col,
@@ -199,7 +200,7 @@ def tile_list_harp_string_adviser_kernel(
                 nc.scalar.activation(gut[:, t, :], gut[:, t, :], ACT.Identity,
                                      bias=cols[:, c : c + 1], scale=gain_m2[:, c : c + 1])
             for h in range(2):
-                acc = psum.tile([P, 2, W], F32, name="test_sum", tag="sums", bufs=6)
+                acc = test_sums[h]
                 for tt in range(2):
                     for a in range(2):
                         col = H * a + 512 * b + P * (2 * h + tt)
@@ -209,7 +210,7 @@ def tile_list_harp_string_adviser_kernel(
             if (s, b) == (0, 0):
                 z = held("wc_bf1", [P, 4 * W], BF16)
             else:
-                z = ring.tile([P, 4 * W], BF16, name="z", tag="turns", align_bytes=64)
+                z = ring.tile([P, 4 * W], BF16, name="z", tag="turns", bufs=2, align_bytes=64)
             nc.vector.tensor_tensor(z[:].rearrange("p (c i t) -> p c t i", i=4, t=4),
                                     test[:].rearrange("p t (c i) -> p c t i", i=4),
                                     gut[:].rearrange("p t (c i) -> p c t i", i=4), ALU.mult)
@@ -226,26 +227,31 @@ def tile_list_harp_string_adviser_kernel(
                 nc.scalar.activation(alone[:, nn, :], acc[:, nn, :], ACT.Identity, bias=cols[:, c : c + 1])
             return alone
 
-        def second_stage(s, h, z_q, alone):
-            js = slice(W * s, W * (s + 1))
-            if True:
-                joint = psum.tile([P, 2, W], F32, name="joint", tag="sums", bufs=6)
-                for nn in range(2):
-                    col = P * (2 * h + nn)
-                    for b in range(2):
-                        mx(joint[:, nn, :], wz_q[b][0][:, col : col + P].bitcast(FP8X4), wz_q[b][1], col,
-                           z_q[b][0], z_q[b][1][:], b == 0, b == 1)
-                y = ring.tile([P, 2, W], F32, name="y", tag="turns", align_bytes=64)
-                nc.vector.tensor_tensor(y[:], joint[:], alone[:], ALU.max)
-                for nn in range(2):
-                    i = 2 * h + nn
-                    nc.vector.tensor_tensor(page[i][:].indirect(list3[:, OC * s : OC * (s + 1)]),
-                                            y[:, nn, :], wgo_sb[:, js], ALU.mult)
-                    if s == SLICES - 1:
-                        nc.sync.dma_start(out=out[P * i : P * (i + 1), :], in_=page[i][:])
+        def joint_sums(s, h, z_q):
+            joint = psum.tile([P, 2, W], F32, name="joint", tag="sums", bufs=6)
+            for nn in range(2):
+                col = P * (2 * h + nn)
+                for b in range(2):
+                    mx(joint[:, nn, :], wz_q[b][0][:, col : col + P].bitcast(FP8X4), wz_q[b][1], col,
+                       z_q[b][0], z_q[b][1][:], b == 0, b == 1)
+            return joint
 
-        z_q, alones = [], []
-        for k in range(2 * SLICES + LAG):
+        def place(s, h, joint, alone):
+            js = slice(W * s, W * (s + 1))
+            ys = []
+            for nn in range(2):
+                y = ring.tile([P, W], F32, name="y", tag="turns", bufs=2, align_bytes=64)
+                nc.vector.tensor_tensor(y[:], joint[:, nn, :], alone[:, nn, :], ALU.max)
+                ys.append(y)
+            for nn in range(2):
+                i = 2 * h + nn
+                nc.vector.tensor_tensor(page[i][:].indirect(list3[:, OC * s : OC * (s + 1)]),
+                                        ys[nn][:], wgo_sb[:, js], ALU.mult)
+                if s == SLICES - 1:
+                    nc.sync.dma_start(out=out[P * i : P * (i + 1), :], in_=page[i][:])
+
+        z_q, alones, joints = [], [], []
+        for k in range(2 * SLICES + 2):
             if k < 2 * SLICES:
                 z_q.append(first_stage(k // 2, k % 2))
                 alones.append(alone_scores(k // 2, k % 2))
@@ -253,6 +259,8 @@ def tile_list_harp_string_adviser_kernel(
                     wz_q.extend(prepare_wz(b) for b in range(2))
                 if k in (1, 3):
                     gather_slice((k + 3) // 2)
-            if k >= LAG:
-                s = (k - LAG) // 2
-                second_stage(s, (k - LAG) % 2, z_q[2 * s : 2 * s + 2], alones[k - LAG])
+            if 1 <= k <= 2 * SLICES:
+                s = (k - 1) // 2
+                joints.append(joint_sums(s, (k - 1) % 2, z_q[2 * s : 2 * s + 2]))
+            if k >= 2:
+                place((k - 2) // 2, k % 2, joints[k - 2], alones[k - 2])

from contextlib import ExitStack

import concourse.mybir as mybir
from concourse.masks import make_identity

F32 = mybir.dt.float32
BF16 = mybir.dt.bfloat16
I32 = mybir.dt.int32
U32 = mybir.dt.uint32
U16 = mybir.dt.uint16
U8 = mybir.dt.uint8
FP8X4 = mybir.dt.float8_e4m3fn_x4
FP4X4 = mybir.dt.float4_e2m1fn_x4
ACT = mybir.ActivationFunctionType
ALU = mybir.AluOpType

FLOPS = 4831838208

P = 128
T = 2048
S = 1024
H = 1024
N = 512
W = 256
SLICES = S // W
OC = W // 16


def tile_list_harp_string_adviser_kernel(
    tc, tab_words, tab_scales, tab2_words, tab2_scales, offs, offs2, offs3, wt_words, wt_scales,
    wb_words, wb_scales, wc, gain, wz, bb, wgo, page1, out,
):
    nc = tc.nc
    with ExitStack() as ctx:
        keep = ctx.enter_context(tc.tile_pool(name="keep", bufs=1))
        ring = ctx.enter_context(tc.tile_pool(name="ring", bufs=3))
        psum = ctx.enter_context(tc.psum_pool(name="psum", bufs=2))

        def held(name, shape, dtype):
            return keep.tile(shape, dtype, name=name, align_bytes=64)

        lists8 = held("lists8", [P, S // 16], U16)
        list2 = held("list2", [P, S // 16], U16)
        list3 = held("list3", [P, S // 16], U16)
        tab_sc = [held("tab_sc%d" % a, [P, T], U8) for a in range(2)]
        tab2_sc = held("tab2_sc", [P, T], U8)
        wt_sc_raw = held("wt_sc_raw", [P, 2 * H], U8)
        wb_sc = held("wb_sc", [P, N], U8)
        v_sc = [held("v_sc%d" % f, [P, 2, S // 2], U8) for f in range(2)]
        rows = held("rows", [P, P], F32)
        ident = held("ident", [P, P], F32)

        warm = held("warm", [P, 1], F32)
        nc.vector.memset(warm[:], 0.0)
        nc.scalar.activation(warm[:], warm[:], ACT.Silu)
        nc.vector.memset(tab_sc[0][:].bitcast(I32), 0)
        nc.gpsimd.memset(tab_sc[1][:].bitcast(I32), 0)
        nc.vector.memset(tab2_sc[:].bitcast(I32), 0)
        nc.gpsimd.memset(wt_sc_raw[:].bitcast(I32), 0)
        nc.gpsimd.memset(rows[:], 0.0)
        nc.vector.memset(wb_sc[:].bitcast(I32), 0)

        make_identity(nc, ident[:])
        for f in range(2):
            nc.vector.memset(v_sc[f][:].rearrange("p a s -> p (a s)").bitcast(I32), 0)
        nc.sync.dma_start(lists8[:], offs)
        for a in range(2):
            nc.sync.dma_start(out=tab_sc[a][:].bitcast(I32)[0:P:8, :], in_=tab_scales[a].bitcast(I32))
        nc.sync.dma_start(list2[:], offs2)
        tab2_w = held("tab2_w", [P, T], I32)
        nc.sync.dma_start(out=tab2_w[:], in_=tab2_words[0].rearrange("p n t -> p (n t)").bitcast(I32))
        for d in range(4):
            nc.scalar.dma_start(out=tab2_sc[:].bitcast(I32)[32 * d : 32 * d + 4, :],
                                in_=tab2_scales[0, 4 * d : 4 * d + 4, :].bitcast(I32))
        for b in range(2):
            nc.scalar.dma_start(
                out=rows[4 * b : 4 * b + 4, :].rearrange("t (u e) -> t u e", e=4),
                in_=gain[512 * b : 512 * (b + 1)].rearrange("(u t e) -> t u e", t=4, e=4))
        nc.scalar.dma_start(out=rows[8:12, :], in_=bb.rearrange("(i p) -> i p", p=P))
        wc_raw = [held("wc_raw%d" % b, [P, 4, 512], F32) for b in range(2)]
        wc_rows = wc.rearrange("(p j) c -> p j c", j=4)
        nc.sync.dma_start(out=wc_raw[0][:], in_=wc_rows[:, :, 0:512])
        for d in range(4):
            nc.gpsimd.dma_start(
                out=wt_sc_raw[:].bitcast(I32)[32 * d : 32 * d + 4, :].rearrange("p (a w) -> p a w", a=2),
                in_=wt_scales.bitcast(I32)[:, 4 * d : 4 * d + 4, :].rearrange("a r w -> r a w"))
        tab_w = [held("tab_w%d" % a, [P, T], I32) for a in range(2)]
        for a in range(2):
            nc.sync.dma_start(out=tab_w[a][:], in_=tab_words[a].rearrange("p n t -> p (n t)").bitcast(I32))
        wt_raw = held("wt_raw", [P, 2, H // 2], I32)
        nc.sync.dma_start(out=wt_raw[:], in_=wt_words.bitcast(I32).rearrange("a p w -> p a w"))
        nc.sync.dma_start(out=wc_raw[1][:], in_=wc_rows[:, :, 512:1024])

        def tab_scale_half(f, queue):
            picked = held("tab_sc_g%d" % f, [P, 2, S // 2], U8)
            for a in range(2):
                nc.vector.tensor_copy(picked[:, a, :], tab_sc[a][:].indirect(lists8[:, 2 * OC * f : 2 * OC * (f + 1)]))
            for r in range(4):
                queue.dma_start(out=v_sc[f][:].rearrange("p a s -> p (a s)").bitcast(I32)[r:P:32, :],
                                in_=picked[:].rearrange("p a s -> p (a s)").bitcast(I32)[8 * r : P : 32, :])

        tab_scale_half(0, nc.scalar)
        wb_w = held("wb_w", [P, N], I32)
        nc.sync.dma_start(out=wb_w[:], in_=wb_words[0].rearrange("p n t -> p (n t)").bitcast(I32))
        for d in range(4):
            nc.sync.dma_start(out=wb_sc[:].bitcast(I32)[32 * d : 32 * d + 4, :],
                                in_=wb_scales[0, 4 * d : 4 * d + 4, :].bitcast(I32))
        nc.sync.dma_start(list3[:], offs3)
        wz_raw = [held("wz_raw%d" % b, [P, 4, N], F32) for b in range(2)]
        for b in (1, 0):
            wz_rows = wz[512 * b : 512 * (b + 1), :].rearrange("(u t e) n -> e u t n", t=4, e=4)
            for e in range(4):
                nc.sync.dma_start(out=wz_raw[b][e:P:4, :, :], in_=wz_rows[e])
        wgo_sb = held("wgo_sb", [P, S], F32)
        nc.sync.dma_start(out=wgo_sb[:], in_=wgo)
        page = [held("page%d" % i, [P, T], F32) for i in range(4)]
        for i in range(4):
            nc.sync.dma_start(out=page[i][:], in_=page1[P * i : P * (i + 1), :])

        def quantise(name, pool, grouped, width):
            codes = pool.tile([P, width], U32, name=name + "_w", align_bytes=64)
            scales = pool.tile([P, width], U8, name=name + "_sc", align_bytes=64)
            nc.vector.quantize_mx(out=codes[:].bitcast(FP8X4), scales=scales[:], in_=grouped)
            return codes, scales

        def prepare_wc(b, copy):
            grouped = held("wc_bf%d" % b, [P, 2048], BF16)
            copy(out=grouped[:].rearrange("p (t u e j) -> p t u j e", t=4, e=4, j=4),
                 in_=wc_raw[b][:].rearrange("p j (u t e) -> p t u j e", t=4, e=4))
            return quantise("wc%d" % b, keep, grouped[:], 512)

        def prepare_wz(b):
            grouped = ring.tile([P, 2048], BF16, name="wz_bf", tag="turns", bufs=2, align_bytes=64)
            nc.vector.tensor_copy(out=grouped[:].rearrange("p (c i t) -> p c t i", i=4, t=4),
                                  in_=wz_raw[b][:].rearrange("p t (c i) -> p c t i", i=4))
            return quantise("wz%d" % b, keep, grouped[:], 512)

        def gather_words(name, window, offsets, s):
            picked = ring.tile([P, W], U32, name=name, bufs=2, align_bytes=64)
            nc.vector.tensor_copy(picked[:], window[:].bitcast(U32).indirect(offsets[:, OC * s : OC * (s + 1)]))
            return picked

        def gather_scales(s):
            picked = ring.tile([P, W], U8, name="v2_sc", bufs=2, align_bytes=64)
            nc.vector.tensor_copy(picked[:], tab2_sc[:].indirect(list2[:, OC * s : OC * (s + 1)]))
            return picked

        v2_w, v_w, v2_sc = {}, {}, {}
        v2_sc[0] = gather_scales(0)
        v2_w[0] = gather_words("v2", tab2_w, list2, 0)
        wc_q = [prepare_wc(0, nc.scalar.copy)]
        wt_w = held("wt_w", [P, 2 * H // 2], I32)
        nc.vector.tensor_copy(out=wt_w[:].rearrange("p (ab t u w) -> p ab t u w", ab=4, t=4, w=2),
                       in_=wt_raw[:].rearrange("p a (b u t w) -> p (a b) t u w", b=2, t=4, w=2))
        wt_sc = held("wt_sc", [P, 2 * H], U8)
        nc.vector.tensor_copy(out=wt_sc[:].bitcast(I32).rearrange("p (ab t u) -> p ab t u", ab=4, t=4),
                       in_=wt_sc_raw[:].bitcast(I32).rearrange("p (ab u t) -> p ab t u", ab=4, t=4))

        turned = psum.tile([P, 2, W], F32, name="alone_sum")
        nc.tensor.transpose(turned[:, 0, 0:P], rows[:], ident[:])
        cols = held("cols", [P, 12], F32)
        nc.scalar.copy(cols[:], turned[:, 0, 0:12])
        gain_m2 = held("gain_m2", [P, 8], F32)
        nc.scalar.activation(gain_m2[:], turned[:, 0, 0:8], ACT.Copy, scale=-2.0)

        for a in range(2):
            v_w[a, 0] = gather_words("v%d" % a, tab_w[a], lists8, 0)
        wc_q.append(prepare_wc(1, nc.vector.tensor_copy))

        def gather_slice(s):
            v2_sc[s] = gather_scales(s)
            v2_w[s] = gather_words("v2", tab2_w, list2, s)
            for a in range(2):
                v_w[a, s] = gather_words("v%d" % a, tab_w[a], lists8, s)

        gather_slice(1)
        tab_scale_half(1, nc.gpsimd)
        wz_q = []

        def mx(acc, codes, scales, col, rhs, rhs_scale, start, stop):
            nc.tensor.matmul_mx(out=acc, lhsT=codes, lhsT_scale=scales[:, col : col + P], rhs=rhs[:].bitcast(FP8X4),
                                rhs_scale=rhs_scale, start=start, stop=stop)

        def first_stage(s, b):
            js = slice(W * s, W * (s + 1))
            test = ring.tile([P, 4, W], F32, name="test")
            gut = ring.tile([P, 4, W], F32, name="gut")
            test_sums = [psum.tile([P, 2, W], F32, name="test_sum", tag="sums", bufs=6) for h in range(2)]
            gut_sums = [psum.tile([P, 2, W], F32, name="gut_sum", tag="sums", bufs=6) for h in range(2)]
            for h in range(2):
                acc = gut_sums[h]
                for tt in range(2):
                    col = P * (2 * h + tt)
                    mx(acc[:, tt, :], wc_q[b][0][:, col : col + P].bitcast(FP8X4), wc_q[b][1], col,
                       v2_w[s], v2_sc[s][:], True, True)
                nc.scalar.activation(gut[:, 2 * h : 2 * h + 2, :], acc[:], ACT.Sin, scale=0.5)
            nc.scalar.activation(gut[:], gut[:], ACT.Square)
            for t in range(4):
                c = 4 * b + t
                nc.scalar.activation(gut[:, t, :], gut[:, t, :], ACT.Identity,
                                     bias=cols[:, c : c + 1], scale=gain_m2[:, c : c + 1])
            for h in range(2):
                acc = test_sums[h]
                for tt in range(2):
                    for a in range(2):
                        col = H * a + 512 * b + P * (2 * h + tt)
                        mx(acc[:, tt, :], wt_w[:].bitcast(U8)[:, 2 * col : 2 * (col + P)].bitcast(FP4X4), wt_sc, col,
                           v_w[a, s], v_sc[s // 2][:, a, W * (s % 2) : W * (s % 2 + 1)], a == 0, a == 1)
                nc.scalar.activation(test[:, 2 * h : 2 * h + 2, :], acc[:], ACT.Tanh)
            if (s, b) == (0, 0):
                z = held("wc_bf1", [P, 4 * W], BF16)
            else:
                z = ring.tile([P, 4 * W], BF16, name="z", tag="turns", bufs=2, align_bytes=64)
            nc.vector.tensor_tensor(z[:].rearrange("p (c i t) -> p c t i", i=4, t=4),
                                    test[:].rearrange("p t (c i) -> p c t i", i=4),
                                    gut[:].rearrange("p t (c i) -> p c t i", i=4), ALU.mult)
            return quantise("z%d" % b, ring, z[:], W)

        def alone_scores(s, h):
            acc = psum.tile([P, 2, W], F32, name="alone_sum")
            alone = ring.tile([P, 2, W], F32, name="alone", bufs=4)
            for nn in range(2):
                col = P * (2 * h + nn)
                mx(acc[:, nn, :], wb_w[:, col : col + P].bitcast(FP8X4), wb_sc, col, v2_w[s], v2_sc[s][:], True, True)
            for nn in range(2):
                c = 8 + 2 * h + nn
                nc.scalar.activation(alone[:, nn, :], acc[:, nn, :], ACT.Identity, bias=cols[:, c : c + 1])
            return alone

        def joint_sums(s, h, z_q):
            joint = psum.tile([P, 2, W], F32, name="joint", tag="sums", bufs=6)
            for nn in range(2):
                col = P * (2 * h + nn)
                for b in range(2):
                    mx(joint[:, nn, :], wz_q[b][0][:, col : col + P].bitcast(FP8X4), wz_q[b][1], col,
                       z_q[b][0], z_q[b][1][:], b == 0, b == 1)
            return joint

        def place(s, h, joint, alone):
            js = slice(W * s, W * (s + 1))
            ys = []
            for nn in range(2):
                y = ring.tile([P, W], F32, name="y", tag="turns", bufs=2, align_bytes=64)
                nc.vector.tensor_tensor(y[:], joint[:, nn, :], alone[:, nn, :], ALU.max)
                ys.append(y)
            for nn in range(2):
                i = 2 * h + nn
                nc.vector.tensor_tensor(page[i][:].indirect(list3[:, OC * s : OC * (s + 1)]),
                                        ys[nn][:], wgo_sb[:, js], ALU.mult)
                if s == SLICES - 1:
                    nc.sync.dma_start(out=out[P * i : P * (i + 1), :], in_=page[i][:])

        z_q, alones, joints = [], [], []
        for k in range(2 * SLICES + 2):
            if k < 2 * SLICES:
                z_q.append(first_stage(k // 2, k % 2))
                alones.append(alone_scores(k // 2, k % 2))
                if k == 1:
                    wz_q.extend(prepare_wz(b) for b in range(2))
                if k in (1, 3):
                    gather_slice((k + 3) // 2)
            if 1 <= k <= 2 * SLICES:
                s = (k - 1) // 2
                joints.append(joint_sums(s, (k - 1) % 2, z_q[2 * s : 2 * s + 2]))
            if k >= 2:
                place((k - 2) // 2, k % 2, joints[k - 2], alones[k - 2])
